import numpy as np
import ml_dtypes


def mxq(x, axis, fmt="e4m3"):
    dtype, down = {"e4m3": (ml_dtypes.float8_e4m3fn, 7), "e5m2": (ml_dtypes.float8_e5m2, 14)}[fmt]
    v = np.moveaxis(np.asarray(x, np.float32).astype(ml_dtypes.bfloat16).astype(np.float64), axis, -1)
    blocks = v.reshape(v.shape[:-1] + (-1, 32))
    amax = np.abs(blocks).max(-1, keepdims=True)
    byte = np.maximum(np.where(amax > 0, np.frexp(amax)[1] - 1 + 127, 0) - down, 1)
    scale = np.exp2(byte - 127.0)
    codes = (blocks / scale).astype(np.float32).astype(dtype).astype(np.float64)
    return np.moveaxis((codes * scale).reshape(v.shape), -1, axis)


WIDE = False


def mx_kscale(k):
    if not WIDE:
        return np.ones(k)
    levels = np.array([10, -10, 5, -5, 0])
    if k % 512:
        return np.exp2(np.random.permutation(np.resize(levels, k // 32))).repeat(32)
    a = np.empty((k // 512, 16))
    for p in range(k // 512):
        a[p, :8] = np.random.permutation(np.resize(levels, 8))
        for g in range(8):
            far = levels[np.abs(levels - a[p, g]) >= 10]
            a[p, g + 8] = far[np.random.randint(len(far))]
    return np.exp2(a.ravel()).repeat(32)


def f64(x):
    return np.asarray(x).astype(np.float64)


def striped(idx):
    return np.tile(idx.reshape(-1, 16).T, (8, 1)).astype(np.uint16)


def unstriped(offs):
    return offs[:16].T.reshape(-1).astype(np.int64)


E2M1 = np.array([0.0, 0.5, 1.0, 1.5, 2.0, 3.0, 4.0, 6.0, -0.0, -0.5, -1.0, -1.5, -2.0, -3.0, -4.0, -6.0])


def pack_weight(w, fmt):
    k, n = w.shape
    w = f64(np.asarray(w, np.float32).astype(ml_dtypes.bfloat16)).reshape(k // 32, 32, n)
    amax = np.abs(w).max(1)
    if fmt == "e4m3":
        byte = np.frexp(amax)[1] - 1 + 127 - 7
    else:
        mant, ex = np.frexp(amax / 6.0)
        byte = np.where(mant > 0.5, ex, ex - 1) + 127
    byte = np.clip(np.where(amax > 0, byte, 1), 1, 254)
    scaled = (w * np.exp2(127.0 - byte)[:, None, :]).reshape(k, n).astype(np.float32)
    by_word = np.ascontiguousarray(scaled.reshape(k // 512, 128, 4, n).transpose(0, 1, 3, 2))
    if fmt == "e4m3":
        words = by_word.astype(ml_dtypes.float8_e4m3fn).view(np.uint8)
    else:
        c = by_word.astype(ml_dtypes.float4_e2m1fn).view(np.uint8) & 0xF
        words = (c[..., 0::2] | (c[..., 1::2] << 4)).reshape(k // 512, 128, 2 * n)
    return np.ascontiguousarray(words), np.ascontiguousarray(byte.astype(np.uint8).reshape(k // 512, 16, n))


def unpack_weight(words, scales, fmt):
    g, _, n = scales.shape
    words = np.ascontiguousarray(words).reshape(g, 128, n, -1)
    if fmt == "e4m3":
        vals = words.view(ml_dtypes.float8_e4m3fn).astype(np.float64)
    else:
        nib = np.empty((g, 128, n, 4), np.uint8)
        nib[..., 0::2] = words & 0xF
        nib[..., 1::2] = words >> 4
        vals = E2M1[nib]
    vals = vals * np.repeat(np.exp2(scales.astype(np.float64) - 127.0), 8, axis=1)[..., None]
    return vals.transpose(0, 1, 3, 2).reshape(g * 512, n)


def gelu(v):
    return 0.5 * v * (1.0 + np.tanh(np.sqrt(2.0 / np.pi) * (v + 0.044715 * v**3)))


K, K2, H, N, T, T3, S, P = 1536, 512, 1024, 384, 4096, 2048, 1024, 512

def setup_inputs():
    n = np.random.standard_normal
    s = mx_kscale(K)[:, None]
    s2 = mx_kscale(K2)[:, None]
    u = mx_kscale(H)[:, None]
    tab_words, tab_scales = pack_weight(n((K, T)) * s, "e4m3")
    tab2_words, tab2_scales = pack_weight(n((K2, T3)) * s2, "e4m3")
    w4_words, w4_scales = pack_weight(1.5 * n((H, N)) / np.sqrt(H) / u, "e2m1")
    return {
        "tab_words": tab_words, "tab_scales": tab_scales,
        "offs": striped(np.random.permutation(T)[:S]),
        "tab2_words": tab2_words, "tab2_scales": tab2_scales,
        "offs2": striped(np.random.permutation(T3)[:P]),
        "pos1": striped(np.random.permutation(S)[:P]),
        "w1": (1.2 * n((K, H)) / np.sqrt(K) / s).astype(np.float32),
        "b1": (0.6 * n(H)).astype(np.float32),
        "gain": (np.exp(0.3 * n(H)) * u[:, 0]).astype(np.float32),
        "w4_words": w4_words, "w4_scales": w4_scales,
        "w2": (0.8 * n((K2, N)) / np.sqrt(K2) / s2).astype(np.float32),
    }

def reference(tab_words, tab_scales, offs, tab2_words, tab2_scales, offs2, pos1,
              w1, b1, gain, w4_words, w4_scales, w2):
    v = unpack_weight(tab_words, tab_scales, "e4m3")[:, unstriped(offs)]
    v2 = unpack_weight(tab2_words, tab2_scales, "e4m3")[:, unstriped(offs2)]
    w4 = unpack_weight(w4_words, w4_scales, "e2m1")
    w1q = mxq(f64(w1), 0, "e4m3")
    h = np.tanh((w1q.T @ v) + f64(b1)[:, None]) * f64(gain)[:, None]
    hq = mxq(h, 0, "e4m3")
    y = w4.T @ hq
    w2q = mxq(f64(w2), 0, "e4m3")
    b = w2q.T @ v2
    return y[:, unstriped(pos1)] + np.exp(b)

@@ -1,0 +1,257 @@
+from contextlib import ExitStack
+
+import concourse.mybir as mybir
+
+K, K2, H, N, T, T3, S, PICK = 1536, 512, 1024, 384, 4096, 2048, 1024, 512
+FLOPS = 2 * (K * H * S + H * N * S + K2 * N * PICK)
+
+F32 = mybir.dt.float32
+BF16 = mybir.dt.bfloat16
+I32 = mybir.dt.int32
+U32 = mybir.dt.uint32
+U16 = mybir.dt.uint16
+U8 = mybir.dt.uint8
+FP8X4 = mybir.dt.float8_e4m3fn_x4
+FP4X4 = mybir.dt.float4_e2m1fn_x4
+ACT = mybir.ActivationFunctionType
+ALU = mybir.AluOpType
+
+P = 128
+PACK = 4
+KP = P * PACK
+PASSES = K // KP
+BLOCKS = H // KP
+NT = N // P
+CH = 256
+CHUNKS = S // CH
+HALF = 512
+LW = 16
+
+
+def tile_list_colic_gut_scores_kernel(
+    tc, tab_words, tab_scales, offs, tab2_words, tab2_scales, offs2, pos1,
+    w1, b1, gain, w4_words, w4_scales, w2, out,
+):
+    nc = tc.nc
+    with ExitStack() as ctx:
+        lists = ctx.enter_context(tc.tile_pool(name="lists", bufs=1))
+        keep = ctx.enter_context(tc.tile_pool(name="keep", bufs=1))
+        ring = ctx.enter_context(tc.tile_pool(name="ring", bufs=3))
+        psum = ctx.enter_context(tc.psum_pool(name="psum", bufs=1))
+
+        offs_t = lists.tile([P, S // LW], U16, name="offs_t")
+        offs2_t = lists.tile([P, PICK // LW], U16, name="offs2_t")
+        pos1_t = lists.tile([P, PICK // LW], U16, name="pos1_t")
+
+        tab_w = [keep.tile([P, T], U32, name=f"tab_w{a}") for a in range(PASSES)]
+        tab_s = keep.tile([P, T], U8, name="tab_s")
+        tab2_w = keep.tile([P, T3], U32, name="tab2_w")
+        tab2_s = keep.tile([P, T3], U8, name="tab2_s")
+        w1_raw = {(b, a): keep.tile([P, PACK, KP], F32, name=f"w1_raw{b}{a}")
+                  for b in range(BLOCKS) for a in range(PASSES)}
+        w2_raw = keep.tile([P, PACK, N], F32, name="w2_raw")
+        w4_w = keep.tile([P, BLOCKS, 2 * N], U8, name="w4_w", align_bytes=64)
+        w4_s = keep.tile([P, BLOCKS, N], U8, name="w4_s", align_bytes=64)
+        b1_t = keep.tile([P, BLOCKS, PACK], F32, name="b1_t")
+        gain_t = keep.tile([P, BLOCKS, PACK], F32, name="gain_t")
+
+        v_w = [keep.tile([P, S], U32, name=f"v_w{a}", align_bytes=64) for a in range(PASSES)]
+        v_s = keep.tile([P, S], U8, name="v_s", align_bytes=64)
+        v2_w = keep.tile([P, PICK], U32, name="v2_w", align_bytes=64)
+        v2_s = keep.tile([P, PICK], U8, name="v2_s", align_bytes=64)
+        w1_c = {(b, a): keep.tile([P, KP], U32, name=f"w1_c{b}{a}", align_bytes=64)
+                for b in range(BLOCKS) for a in range(PASSES)}
+        w1_s = {(b, a): keep.tile([P, KP], U8, name=f"w1_s{b}{a}", align_bytes=64)
+                for b in range(BLOCKS) for a in range(PASSES)}
+        w2_c = keep.tile([P, N], U32, name="w2_c", align_bytes=64)
+        w2_s = keep.tile([P, N], U8, name="w2_s", align_bytes=64)
+        h_c = [keep.tile([P, S], U32, name=f"h_c{b}", align_bytes=64) for b in range(BLOCKS)]
+        h_s = [keep.tile([P, S], U8, name=f"h_s{b}", align_bytes=64) for b in range(BLOCKS)]
+        y_t = [keep.tile([P, S], F32, name=f"y_t{n}") for n in range(NT)]
+        e_t = [keep.tile([P, PICK], F32, name=f"e_t{n}") for n in range(NT)]
+        o_t = [keep.tile([P, PICK], F32, name=f"o_t{n}") for n in range(NT)]
+
+        def bank(i, name):
+            return psum.tile([P, HALF], F32, name=name, tag=f"bank{i}")
+
+        nc.vector.memset(tab_s[:].bitcast(I32), 0)
+        nc.vector.memset(tab2_s[:].bitcast(I32), 0)
+        nc.vector.memset(w4_s[:].rearrange("p a n -> p (a n)").bitcast(I32), 0)
+
+        def load_tab(a):
+            nc.sync.dma_start(tab_w[a][:].bitcast(I32),
+                              tab_words[a].rearrange("p t i -> p (t i)").bitcast(I32))
+
+        def load_w1(b, a):
+            rows = w1[a * KP:(a + 1) * KP, b * KP:(b + 1) * KP]
+            nc.sync.dma_start(w1_raw[b, a][:], rows.rearrange("(p j) c -> p j c", j=PACK))
+
+        nc.sync.dma_start(offs_t[:], offs)
+        load_w1(0, 0)
+        load_tab(0)
+        for q in range(4):
+            nc.sync.dma_start(tab_s[32 * q:32 * q + 4 * PASSES, :].bitcast(I32),
+                              tab_scales[:, 4 * q:4 * q + 4, :].bitcast(I32))
+        nc.sync.dma_start(b1_t[:], b1.rearrange("(b p t) -> p b t", p=P, t=PACK))
+        load_w1(0, 1)
+        nc.sync.dma_start(gain_t[:], gain.rearrange("(b p t) -> p b t", p=P, t=PACK))
+        load_tab(1)
+        for q in range(4):
+            nc.sync.dma_start(tab2_s[32 * q:32 * q + 4, :].bitcast(I32),
+                              tab2_scales[0, 4 * q:4 * q + 4, :].bitcast(I32))
+        nc.sync.dma_start(offs2_t[:], offs2)
+        load_w1(0, 2)
+        load_tab(2)
+        load_w1(1, 0)
+        for q in range(4):
+            nc.sync.dma_start(w4_s[32 * q:32 * q + 4, :, :].bitcast(I32),
+                              w4_scales[:, 4 * q:4 * q + 4, :].rearrange("a r n -> r a n").bitcast(I32))
+        nc.sync.dma_start(w4_w[:].bitcast(I32), w4_words.rearrange("a p c -> p a c").bitcast(I32))
+        nc.sync.dma_start(pos1_t[:], pos1)
+        load_w1(1, 1)
+        load_w1(1, 2)
+        nc.sync.dma_start(w2_raw[:], w2.rearrange("(p j) c -> p j c", j=PACK))
+        nc.sync.dma_start(tab2_w[:].bitcast(I32),
+                          tab2_words[0].rearrange("p t i -> p (t i)").bitcast(I32))
+
+        w1_b = {}
+
+        def round_w1(b, a, copy):
+            grouped = ring.tile([P, PACK * KP], BF16, name="w1_b", align_bytes=64)
+            w1_b[b, a] = grouped
+            copy(grouped[:].rearrange("p (t m j) -> p m j t", t=PACK, j=PACK),
+                 w1_raw[b, a][:].rearrange("p j (m t) -> p m j t", t=PACK))
+
+        def quant_w1(b, a):
+            nc.vector.quantize_mx(out=w1_c[b, a][:].bitcast(FP8X4), scales=w1_s[b, a][:], in_=w1_b[b, a][:])
+
+        def gather_words(a, c0, c1):
+            nc.vector.tensor_copy(v_w[a][:, c0:c1], tab_w[a][:].indirect(offs_t[:, c0 // LW:c1 // LW]))
+
+        acc = {}
+
+        def stage1(b, a, c):
+            cols = slice(c * CH, (c + 1) * CH)
+            for t in range(PACK):
+                if a == 0 and t % 2 == 0:
+                    acc[b, c, t // 2] = bank(2 * c + t // 2, f"h{b}{c}{t // 2}")
+                nc.tensor.matmul_mx(
+                    out=acc[b, c, t // 2][:, (t % 2) * CH:(t % 2 + 1) * CH],
+                    lhsT=w1_c[b, a][:, t * P:(t + 1) * P].bitcast(FP8X4),
+                    lhsT_scale=w1_s[b, a][:, t * P:(t + 1) * P],
+                    rhs=v_w[a][:, cols].bitcast(FP8X4),
+                    rhs_scale=v_s[4 * a:P, cols],
+                    start=(a == 0 and t % 2 == 0),
+                    stop=(a == PASSES - 1 and t % 2 == 1),
+                )
+
+        th = {}
+
+        def tanh(b, c):
+            th[b, c] = ring.tile([P, PACK, CH], F32, name="th", bufs=5)
+            for t in range(PACK):
+                nc.scalar.activation(out=th[b, c][:, t, :],
+                                     in_=acc[b, c, t // 2][:, (t % 2) * CH:(t % 2 + 1) * CH],
+                                     func=ACT.Tanh, bias=b1_t[:, b, t:t + 1])
+
+        hb = {}
+
+        def scale_h(b, c):
+            hb[b, c] = ring.tile([P, PACK * CH], BF16, name="hb", align_bytes=64)
+            g = gain_t[:, b, :].unsqueeze(1).unsqueeze(3).to_broadcast([P, CH // 4, PACK, 4])
+            nc.vector.tensor_tensor(
+                hb[b, c][:].rearrange("p (c i t) -> p c t i", i=4, t=PACK),
+                th[b, c][:].rearrange("p t (c i) -> p c t i", i=4), g, ALU.mult)
+
+        def quant_h(b, c):
+            cols = slice(c * CH, (c + 1) * CH)
+            nc.vector.quantize_mx(out=h_c[b][:, cols].bitcast(FP8X4), scales=h_s[b][:, cols], in_=hb[b, c][:])
+
+        yacc = {}
+
+        def stage2(n, b, c0, c1, start, stop):
+            half = c0 // HALF
+            nc.tensor.matmul_mx(
+                out=yacc[n, half][:, c0 - half * HALF:c1 - half * HALF],
+                lhsT=w4_w[:, b, 2 * n * P:2 * (n + 1) * P].bitcast(FP4X4),
+                lhsT_scale=w4_s[:, b, n * P:(n + 1) * P],
+                rhs=h_c[b][:, c0:c1].bitcast(FP8X4),
+                rhs_scale=h_s[b][:, c0:c1],
+                start=start, stop=stop,
+            )
+
+        round_w1(0, 0, nc.scalar.copy)
+        quant_w1(0, 0)
+        gather_words(0, 0, S)
+        nc.vector.tensor_copy(v_s[:], tab_s[:].indirect(offs_t[:]))
+        round_w1(0, 1, nc.scalar.copy)
+        quant_w1(0, 1)
+        gather_words(1, 0, S)
+        nc.vector.tensor_copy(v2_s[:], tab2_s[:].indirect(offs2_t[:]))
+        round_w1(0, 2, nc.scalar.copy)
+        quant_w1(0, 2)
+        for a in range(PASSES - 1):
+            for c in range(CHUNKS):
+                stage1(0, a, c)
+
+        for c in range(CHUNKS):
+            gather_words(2, c * CH, (c + 1) * CH)
+            stage1(0, 2, c)
+            tanh(0, c)
+        round_w1(1, 0, nc.vector.tensor_copy)
+        scale_h(0, 0)
+        quant_w1(1, 0)
+        round_w1(1, 1, nc.scalar.copy)
+        scale_h(0, 1)
+        quant_h(0, 0)
+        round_w1(1, 2, nc.vector.tensor_copy)
+        quant_w1(1, 1)
+        quant_h(0, 1)
+        quant_w1(1, 2)
+        for a in range(PASSES - 1):
+            for c in range(CHUNKS):
+                stage1(1, a, c)
+
+        w2_b = keep.tile([P, PACK * N], BF16, name="w2_b", align_bytes=64)
+        nc.scalar.copy(w2_b[:].rearrange("p (c i j) -> p c j i", i=4, j=PACK),
+                       w2_raw[:].rearrange("p j (c i) -> p c j i", i=4))
+        for c in range(CHUNKS):
+            stage1(1, 2, c)
+            tanh(1, c)
+        scale_h(0, 2)
+        scale_h(0, 3)
+        quant_h(0, 2)
+        nc.vector.quantize_mx(out=w2_c[:].bitcast(FP8X4), scales=w2_s[:], in_=w2_b[:])
+        quant_h(0, 3)
+        nc.vector.tensor_copy(v2_w[:], tab2_w[:].indirect(offs2_t[:]))
+
+        for n in range(NT):
+            bacc_n = bank(n, f"b{n}")
+            nc.tensor.matmul_mx(
+                out=bacc_n[:],
+                lhsT=w2_c[:, n * P:(n + 1) * P].bitcast(FP8X4),
+                lhsT_scale=w2_s[:, n * P:(n + 1) * P],
+                rhs=v2_w[:].bitcast(FP8X4), rhs_scale=v2_s[:],
+                start=True, stop=True,
+            )
+            nc.scalar.activation(out=e_t[n][:], in_=bacc_n[:], func=ACT.Exp)
+
+        y_banks = {0: (3, 4, 5), 1: (6, 7, 0)}
+        scale_h(1, 0)
+        for c in range(CHUNKS):
+            if c + 1 < CHUNKS:
+                scale_h(1, c + 1)
+            quant_h(1, c)
+            half = c // 2
+            if c % 2 == 0:
+                for n in range(NT):
+                    yacc[n, half] = bank(y_banks[half][n], f"y{n}{half}")
+                    stage2(n, 0, half * HALF, (half + 1) * HALF, True, False)
+            for n in range(NT):
+                stage2(n, 1, c * CH, (c + 1) * CH, False, c % 2 == 1)
+                if c % 2 == 1:
+                    nc.scalar.copy(y_t[n][:, half * HALF:(half + 1) * HALF], yacc[n, half][:])
+
+        for n in range(NT):
+            nc.vector.tensor_tensor(o_t[n][:], y_t[n][:].indirect(pos1_t[:]), e_t[n][:], ALU.add)
+            nc.sync.dma_start(out[n * P:(n + 1) * P, :], o_t[n][:])

@@ -26,6 +26,7 @@ CH = 256
 CHUNKS = S // CH
 HALF = 512
 LW = 16
+LAST_PASS = (2, 1)
 
 
 def tile_list_colic_gut_scores_kernel(
@@ -57,7 +58,6 @@ def tile_list_colic_gut_scores_kernel(
 
         v_w = [keep.tile([P, S], U32, name=f"v_w{a}", align_bytes=64) for a in range(PASSES)]
         v_s = keep.tile([P, S], U8, name="v_s", align_bytes=64)
-        v2_w = keep.tile([P, PICK], U32, name="v2_w", align_bytes=64)
         v2_s = keep.tile([P, PICK], U8, name="v2_s", align_bytes=64)
         w1_c = {(b, a): keep.tile([P, KP], U32, name=f"w1_c{b}{a}", align_bytes=64)
                 for b in range(BLOCKS) for a in range(PASSES)}
@@ -86,38 +86,41 @@ def tile_list_colic_gut_scores_kernel(
             rows = w1[a * KP:(a + 1) * KP, b * KP:(b + 1) * KP]
             nc.sync.dma_start(w1_raw[b, a][:], rows.rearrange("(p j) c -> p j c", j=PACK))
 
-        nc.sync.dma_start(offs_t[:], offs)
         load_w1(0, 0)
         load_tab(0)
-        for q in range(4):
-            nc.sync.dma_start(tab_s[32 * q:32 * q + 4 * PASSES, :].bitcast(I32),
-                              tab_scales[:, 4 * q:4 * q + 4, :].bitcast(I32))
-        nc.sync.dma_start(b1_t[:], b1.rearrange("(b p t) -> p b t", p=P, t=PACK))
-        load_w1(0, 1)
-        nc.sync.dma_start(gain_t[:], gain.rearrange("(b p t) -> p b t", p=P, t=PACK))
-        load_tab(1)
-        for q in range(4):
-            nc.sync.dma_start(tab2_s[32 * q:32 * q + 4, :].bitcast(I32),
-                              tab2_scales[0, 4 * q:4 * q + 4, :].bitcast(I32))
+        nc.sync.dma_start(offs_t[:], offs)
         nc.sync.dma_start(offs2_t[:], offs2)
+        load_w1(0, 1)
+        load_tab(1)
+        nc.sync.dma_start(b1_t[:], b1.rearrange("(b p t) -> p b t", p=P, t=PACK))
+        nc.sync.dma_start(gain_t[:], gain.rearrange("(b p t) -> p b t", p=P, t=PACK))
         load_w1(0, 2)
         load_tab(2)
-        load_w1(1, 0)
-        for q in range(4):
-            nc.sync.dma_start(w4_s[32 * q:32 * q + 4, :, :].bitcast(I32),
-                              w4_scales[:, 4 * q:4 * q + 4, :].rearrange("a r n -> r a n").bitcast(I32))
-        nc.sync.dma_start(w4_w[:].bitcast(I32), w4_words.rearrange("a p c -> p a c").bitcast(I32))
-        nc.sync.dma_start(pos1_t[:], pos1)
-        load_w1(1, 1)
-        load_w1(1, 2)
+        for a in range(PASSES):
+            load_w1(1, a)
         nc.sync.dma_start(w2_raw[:], w2.rearrange("(p j) c -> p j c", j=PACK))
         nc.sync.dma_start(tab2_w[:].bitcast(I32),
                           tab2_words[0].rearrange("p t i -> p (t i)").bitcast(I32))
+        nc.sync.dma_start(w4_w[:].bitcast(I32), w4_words.rearrange("a p c -> p a c").bitcast(I32))
+        nc.sync.dma_start(pos1_t[:], pos1)
+
+        for q in range(4):
+            nc.gpsimd.dma_start(tab_s[32 * q:32 * q + 4 * PASSES, :].bitcast(I32),
+                                tab_scales[:, 4 * q:4 * q + 4, :].bitcast(I32))
+        for q in range(4):
+            nc.gpsimd.dma_start(tab2_s[32 * q:32 * q + 4, :].bitcast(I32),
+                                tab2_scales[0, 4 * q:4 * q + 4, :].bitcast(I32))
+        for q in range(4):
+            nc.gpsimd.dma_start(w4_s[32 * q:32 * q + 4, :, :].bitcast(I32),
+                                w4_scales[:, 4 * q:4 * q + 4, :].rearrange("a r n -> r a n").bitcast(I32))
 
         w1_b = {}
 
         def round_w1(b, a, copy):
-            grouped = ring.tile([P, PACK * KP], BF16, name="w1_b", align_bytes=64)
+            if (b, a) == (1, 1):
+                grouped = keep.tile([P, PACK * KP], BF16, name="w1_b_last", tag="last", align_bytes=64)
+            else:
+                grouped = ring.tile([P, PACK * KP], BF16, name="w1_b", align_bytes=64)
             w1_b[b, a] = grouped
             copy(grouped[:].rearrange("p (t m j) -> p m j t", t=PACK, j=PACK),
                  w1_raw[b, a][:].rearrange("p j (m t) -> p m j t", t=PACK))
@@ -142,7 +145,7 @@ def tile_list_colic_gut_scores_kernel(
                     rhs=v_w[a][:, cols].bitcast(FP8X4),
                     rhs_scale=v_s[4 * a:P, cols],
                     start=(a == 0 and t % 2 == 0),
-                    stop=(a == PASSES - 1 and t % 2 == 1),
+                    stop=(a == LAST_PASS[b] and t % 2 == 1),
                 )
 
         th = {}
@@ -203,26 +206,27 @@ def tile_list_colic_gut_scores_kernel(
         quant_w1(1, 0)
         round_w1(1, 1, nc.scalar.copy)
         scale_h(0, 1)
-        quant_h(0, 0)
         round_w1(1, 2, nc.vector.tensor_copy)
+        quant_h(0, 0)
+        quant_w1(1, 2)
         quant_w1(1, 1)
         quant_h(0, 1)
-        quant_w1(1, 2)
-        for a in range(PASSES - 1):
-            for c in range(CHUNKS):
-                stage1(1, a, c)
+        for c in range(CHUNKS):
+            stage1(1, 0, c)
 
         w2_b = keep.tile([P, PACK * N], BF16, name="w2_b", align_bytes=64)
         nc.scalar.copy(w2_b[:].rearrange("p (c i j) -> p c j i", i=4, j=PACK),
                        w2_raw[:].rearrange("p j (c i) -> p c j i", i=4))
         for c in range(CHUNKS):
             stage1(1, 2, c)
+            stage1(1, 1, c)
             tanh(1, c)
         scale_h(0, 2)
         scale_h(0, 3)
         quant_h(0, 2)
         nc.vector.quantize_mx(out=w2_c[:].bitcast(FP8X4), scales=w2_s[:], in_=w2_b[:])
         quant_h(0, 3)
+        v2_w = keep.tile([P, PICK], U32, name="v2_w", tag="last", align_bytes=64)
         nc.vector.tensor_copy(v2_w[:], tab2_w[:].indirect(offs2_t[:]))
 
         for n in range(NT):
@@ -253,5 +257,9 @@ def tile_list_colic_gut_scores_kernel(
                     nc.scalar.copy(y_t[n][:, half * HALF:(half + 1) * HALF], yacc[n, half][:])
 
         for n in range(NT):
-            nc.vector.tensor_tensor(o_t[n][:], y_t[n][:].indirect(pos1_t[:]), e_t[n][:], ALU.add)
-            nc.sync.dma_start(out[n * P:(n + 1) * P, :], o_t[n][:])
+            step = PICK if n + 1 < NT else PICK // 2
+            for j0 in range(0, PICK, step):
+                cols = slice(j0, j0 + step)
+                nc.vector.tensor_tensor(o_t[n][:, cols], y_t[n][:].indirect(pos1_t[:, j0 // LW:(j0 + step) // LW]),
+                                        e_t[n][:, cols], ALU.add)
+                nc.sync.dma_start(out[n * P:(n + 1) * P, cols], o_t[n][:, cols])

from contextlib import ExitStack

import concourse.mybir as mybir

K, K2, H, N, T, T3, S, PICK = 1536, 512, 1024, 384, 4096, 2048, 1024, 512
FLOPS = 2 * (K * H * S + H * N * S + K2 * N * PICK)

F32 = mybir.dt.float32
BF16 = mybir.dt.bfloat16
I32 = mybir.dt.int32
U32 = mybir.dt.uint32
U16 = mybir.dt.uint16
U8 = mybir.dt.uint8
FP8X4 = mybir.dt.float8_e4m3fn_x4
FP4X4 = mybir.dt.float4_e2m1fn_x4
ACT = mybir.ActivationFunctionType
ALU = mybir.AluOpType

P = 128
PACK = 4
KP = P * PACK
PASSES = K // KP
BLOCKS = H // KP
NT = N // P
CH = 256
CHUNKS = S // CH
HALF = 512
LW = 16
LAST_PASS = (2, 1)


def tile_list_colic_gut_scores_kernel(
    tc, tab_words, tab_scales, offs, tab2_words, tab2_scales, offs2, pos1,
    w1, b1, gain, w4_words, w4_scales, w2, out,
):
    nc = tc.nc
    with ExitStack() as ctx:
        lists = ctx.enter_context(tc.tile_pool(name="lists", bufs=1))
        keep = ctx.enter_context(tc.tile_pool(name="keep", bufs=1))
        ring = ctx.enter_context(tc.tile_pool(name="ring", bufs=3))
        psum = ctx.enter_context(tc.psum_pool(name="psum", bufs=1))

        offs_t = lists.tile([P, S // LW], U16, name="offs_t")
        offs2_t = lists.tile([P, PICK // LW], U16, name="offs2_t")
        pos1_t = lists.tile([P, PICK // LW], U16, name="pos1_t")

        tab_w = [keep.tile([P, T], U32, name=f"tab_w{a}") for a in range(PASSES)]
        tab_s = keep.tile([P, T], U8, name="tab_s")
        tab2_w = keep.tile([P, T3], U32, name="tab2_w")
        tab2_s = keep.tile([P, T3], U8, name="tab2_s")
        w1_raw = {(b, a): keep.tile([P, PACK, KP], F32, name=f"w1_raw{b}{a}")
                  for b in range(BLOCKS) for a in range(PASSES)}
        w2_raw = keep.tile([P, PACK, N], F32, name="w2_raw")
        w4_w = keep.tile([P, BLOCKS, 2 * N], U8, name="w4_w", align_bytes=64)
        w4_s = keep.tile([P, BLOCKS, N], U8, name="w4_s", align_bytes=64)
        b1_t = keep.tile([P, BLOCKS, PACK], F32, name="b1_t")
        gain_t = keep.tile([P, BLOCKS, PACK], F32, name="gain_t")

        v_w = [keep.tile([P, S], U32, name=f"v_w{a}", align_bytes=64) for a in range(PASSES)]
        v_s = keep.tile([P, S], U8, name="v_s", align_bytes=64)
        v2_s = keep.tile([P, PICK], U8, name="v2_s", align_bytes=64)
        w1_c = {(b, a): keep.tile([P, KP], U32, name=f"w1_c{b}{a}", align_bytes=64)
                for b in range(BLOCKS) for a in range(PASSES)}
        w1_s = {(b, a): keep.tile([P, KP], U8, name=f"w1_s{b}{a}", align_bytes=64)
                for b in range(BLOCKS) for a in range(PASSES)}
        w2_c = keep.tile([P, N], U32, name="w2_c", align_bytes=64)
        w2_s = keep.tile([P, N], U8, name="w2_s", align_bytes=64)
        h_c = [keep.tile([P, S], U32, name=f"h_c{b}", align_bytes=64) for b in range(BLOCKS)]
        h_s = [keep.tile([P, S], U8, name=f"h_s{b}", align_bytes=64) for b in range(BLOCKS)]
        y_t = [keep.tile([P, S], F32, name=f"y_t{n}") for n in range(NT)]
        e_t = [keep.tile([P, PICK], F32, name=f"e_t{n}") for n in range(NT)]
        o_t = [keep.tile([P, PICK], F32, name=f"o_t{n}") for n in range(NT)]

        def bank(i, name):
            return psum.tile([P, HALF], F32, name=name, tag=f"bank{i}")

        nc.vector.memset(tab_s[:].bitcast(I32), 0)
        nc.vector.memset(tab2_s[:].bitcast(I32), 0)
        nc.vector.memset(w4_s[:].rearrange("p a n -> p (a n)").bitcast(I32), 0)

        def load_tab(a):
            nc.sync.dma_start(tab_w[a][:].bitcast(I32),
                              tab_words[a].rearrange("p t i -> p (t i)").bitcast(I32))

        def load_w1(b, a):
            rows = w1[a * KP:(a + 1) * KP, b * KP:(b + 1) * KP]
            nc.sync.dma_start(w1_raw[b, a][:], rows.rearrange("(p j) c -> p j c", j=PACK))

        load_w1(0, 0)
        load_tab(0)
        nc.sync.dma_start(offs_t[:], offs)
        nc.sync.dma_start(offs2_t[:], offs2)
        load_w1(0, 1)
        load_tab(1)
        nc.sync.dma_start(b1_t[:], b1.rearrange("(b p t) -> p b t", p=P, t=PACK))
        nc.sync.dma_start(gain_t[:], gain.rearrange("(b p t) -> p b t", p=P, t=PACK))
        load_w1(0, 2)
        load_tab(2)
        for a in range(PASSES):
            load_w1(1, a)
        nc.sync.dma_start(w2_raw[:], w2.rearrange("(p j) c -> p j c", j=PACK))
        nc.sync.dma_start(tab2_w[:].bitcast(I32),
                          tab2_words[0].rearrange("p t i -> p (t i)").bitcast(I32))
        nc.sync.dma_start(w4_w[:].bitcast(I32), w4_words.rearrange("a p c -> p a c").bitcast(I32))
        nc.sync.dma_start(pos1_t[:], pos1)

        for q in range(4):
            nc.gpsimd.dma_start(tab_s[32 * q:32 * q + 4 * PASSES, :].bitcast(I32),
                                tab_scales[:, 4 * q:4 * q + 4, :].bitcast(I32))
        for q in range(4):
            nc.gpsimd.dma_start(tab2_s[32 * q:32 * q + 4, :].bitcast(I32),
                                tab2_scales[0, 4 * q:4 * q + 4, :].bitcast(I32))
        for q in range(4):
            nc.gpsimd.dma_start(w4_s[32 * q:32 * q + 4, :, :].bitcast(I32),
                                w4_scales[:, 4 * q:4 * q + 4, :].rearrange("a r n -> r a n").bitcast(I32))

        w1_b = {}

        def round_w1(b, a, copy):
            if (b, a) == (1, 1):
                grouped = keep.tile([P, PACK * KP], BF16, name="w1_b_last", tag="last", align_bytes=64)
            else:
                grouped = ring.tile([P, PACK * KP], BF16, name="w1_b", align_bytes=64)
            w1_b[b, a] = grouped
            copy(grouped[:].rearrange("p (t m j) -> p m j t", t=PACK, j=PACK),
                 w1_raw[b, a][:].rearrange("p j (m t) -> p m j t", t=PACK))

        def quant_w1(b, a):
            nc.vector.quantize_mx(out=w1_c[b, a][:].bitcast(FP8X4), scales=w1_s[b, a][:], in_=w1_b[b, a][:])

        def gather_words(a, c0, c1):
            nc.vector.tensor_copy(v_w[a][:, c0:c1], tab_w[a][:].indirect(offs_t[:, c0 // LW:c1 // LW]))

        acc = {}

        def stage1(b, a, c):
            cols = slice(c * CH, (c + 1) * CH)
            for t in range(PACK):
                if a == 0 and t % 2 == 0:
                    acc[b, c, t // 2] = bank(2 * c + t // 2, f"h{b}{c}{t // 2}")
                nc.tensor.matmul_mx(
                    out=acc[b, c, t // 2][:, (t % 2) * CH:(t % 2 + 1) * CH],
                    lhsT=w1_c[b, a][:, t * P:(t + 1) * P].bitcast(FP8X4),
                    lhsT_scale=w1_s[b, a][:, t * P:(t + 1) * P],
                    rhs=v_w[a][:, cols].bitcast(FP8X4),
                    rhs_scale=v_s[4 * a:P, cols],
                    start=(a == 0 and t % 2 == 0),
                    stop=(a == LAST_PASS[b] and t % 2 == 1),
                )

        th = {}

        def tanh(b, c):
            th[b, c] = ring.tile([P, PACK, CH], F32, name="th", bufs=5)
            for t in range(PACK):
                nc.scalar.activation(out=th[b, c][:, t, :],
                                     in_=acc[b, c, t // 2][:, (t % 2) * CH:(t % 2 + 1) * CH],
                                     func=ACT.Tanh, bias=b1_t[:, b, t:t + 1])

        hb = {}

        def scale_h(b, c):
            hb[b, c] = ring.tile([P, PACK * CH], BF16, name="hb", align_bytes=64)
            g = gain_t[:, b, :].unsqueeze(1).unsqueeze(3).to_broadcast([P, CH // 4, PACK, 4])
            nc.vector.tensor_tensor(
                hb[b, c][:].rearrange("p (c i t) -> p c t i", i=4, t=PACK),
                th[b, c][:].rearrange("p t (c i) -> p c t i", i=4), g, ALU.mult)

        def quant_h(b, c):
            cols = slice(c * CH, (c + 1) * CH)
            nc.vector.quantize_mx(out=h_c[b][:, cols].bitcast(FP8X4), scales=h_s[b][:, cols], in_=hb[b, c][:])

        yacc = {}

        def stage2(n, b, c0, c1, start, stop):
            half = c0 // HALF
            nc.tensor.matmul_mx(
                out=yacc[n, half][:, c0 - half * HALF:c1 - half * HALF],
                lhsT=w4_w[:, b, 2 * n * P:2 * (n + 1) * P].bitcast(FP4X4),
                lhsT_scale=w4_s[:, b, n * P:(n + 1) * P],
                rhs=h_c[b][:, c0:c1].bitcast(FP8X4),
                rhs_scale=h_s[b][:, c0:c1],
                start=start, stop=stop,
            )

        round_w1(0, 0, nc.scalar.copy)
        quant_w1(0, 0)
        gather_words(0, 0, S)
        nc.vector.tensor_copy(v_s[:], tab_s[:].indirect(offs_t[:]))
        round_w1(0, 1, nc.scalar.copy)
        quant_w1(0, 1)
        gather_words(1, 0, S)
        nc.vector.tensor_copy(v2_s[:], tab2_s[:].indirect(offs2_t[:]))
        round_w1(0, 2, nc.scalar.copy)
        quant_w1(0, 2)
        for a in range(PASSES - 1):
            for c in range(CHUNKS):
                stage1(0, a, c)

        for c in range(CHUNKS):
            gather_words(2, c * CH, (c + 1) * CH)
            stage1(0, 2, c)
            tanh(0, c)
        round_w1(1, 0, nc.vector.tensor_copy)
        scale_h(0, 0)
        quant_w1(1, 0)
        round_w1(1, 1, nc.scalar.copy)
        scale_h(0, 1)
        round_w1(1, 2, nc.vector.tensor_copy)
        quant_h(0, 0)
        quant_w1(1, 2)
        quant_w1(1, 1)
        quant_h(0, 1)
        for c in range(CHUNKS):
            stage1(1, 0, c)

        w2_b = keep.tile([P, PACK * N], BF16, name="w2_b", align_bytes=64)
        nc.scalar.copy(w2_b[:].rearrange("p (c i j) -> p c j i", i=4, j=PACK),
                       w2_raw[:].rearrange("p j (c i) -> p c j i", i=4))
        for c in range(CHUNKS):
            stage1(1, 2, c)
            stage1(1, 1, c)
            tanh(1, c)
        scale_h(0, 2)
        scale_h(0, 3)
        quant_h(0, 2)
        nc.vector.quantize_mx(out=w2_c[:].bitcast(FP8X4), scales=w2_s[:], in_=w2_b[:])
        quant_h(0, 3)
        v2_w = keep.tile([P, PICK], U32, name="v2_w", tag="last", align_bytes=64)
        nc.vector.tensor_copy(v2_w[:], tab2_w[:].indirect(offs2_t[:]))

        for n in range(NT):
            bacc_n = bank(n, f"b{n}")
            nc.tensor.matmul_mx(
                out=bacc_n[:],
                lhsT=w2_c[:, n * P:(n + 1) * P].bitcast(FP8X4),
                lhsT_scale=w2_s[:, n * P:(n + 1) * P],
                rhs=v2_w[:].bitcast(FP8X4), rhs_scale=v2_s[:],
                start=True, stop=True,
            )
            nc.scalar.activation(out=e_t[n][:], in_=bacc_n[:], func=ACT.Exp)

        y_banks = {0: (3, 4, 5), 1: (6, 7, 0)}
        scale_h(1, 0)
        for c in range(CHUNKS):
            if c + 1 < CHUNKS:
                scale_h(1, c + 1)
            quant_h(1, c)
            half = c // 2
            if c % 2 == 0:
                for n in range(NT):
                    yacc[n, half] = bank(y_banks[half][n], f"y{n}{half}")
                    stage2(n, 0, half * HALF, (half + 1) * HALF, True, False)
            for n in range(NT):
                stage2(n, 1, c * CH, (c + 1) * CH, False, c % 2 == 1)
                if c % 2 == 1:
                    nc.scalar.copy(y_t[n][:, half * HALF:(half + 1) * HALF], yacc[n, half][:])

        for n in range(NT):
            step = PICK if n + 1 < NT else PICK // 2
            for j0 in range(0, PICK, step):
                cols = slice(j0, j0 + step)
                nc.vector.tensor_tensor(o_t[n][:, cols], y_t[n][:].indirect(pos1_t[:, j0 // LW:(j0 + step) // LW]),
                                        e_t[n][:, cols], ALU.add)
                nc.sync.dma_start(out[n * P:(n + 1) * P, cols], o_t[n][:, cols])
